import numpy as np
import ml_dtypes


def mxq(x, axis, fmt="e4m3"):
    dtype, down = {"e4m3": (ml_dtypes.float8_e4m3fn, 7), "e5m2": (ml_dtypes.float8_e5m2, 14)}[fmt]
    v = np.moveaxis(np.asarray(x, np.float32).astype(ml_dtypes.bfloat16).astype(np.float64), axis, -1)
    blocks = v.reshape(v.shape[:-1] + (-1, 32))
    amax = np.abs(blocks).max(-1, keepdims=True)
    byte = np.maximum(np.where(amax > 0, np.frexp(amax)[1] - 1 + 127, 0) - down, 1)
    scale = np.exp2(byte - 127.0)
    codes = (blocks / scale).astype(np.float32).astype(dtype).astype(np.float64)
    return np.moveaxis((codes * scale).reshape(v.shape), -1, axis)


WIDE = False


def mx_kscale(k):
    if not WIDE:
        return np.ones(k)
    levels = np.array([10, -10, 5, -5, 0])
    if k % 512:
        return np.exp2(np.random.permutation(np.resize(levels, k // 32))).repeat(32)
    a = np.empty((k // 512, 16))
    for p in range(k // 512):
        a[p, :8] = np.random.permutation(np.resize(levels, 8))
        for g in range(8):
            far = levels[np.abs(levels - a[p, g]) >= 10]
            a[p, g + 8] = far[np.random.randint(len(far))]
    return np.exp2(a.ravel()).repeat(32)


def f64(x):
    return np.asarray(x).astype(np.float64)


def striped(idx):
    return np.tile(idx.reshape(-1, 16).T, (8, 1)).astype(np.uint16)


def unstriped(offs):
    return offs[:16].T.reshape(-1).astype(np.int64)


E2M1 = np.array([0.0, 0.5, 1.0, 1.5, 2.0, 3.0, 4.0, 6.0, -0.0, -0.5, -1.0, -1.5, -2.0, -3.0, -4.0, -6.0])


def pack_weight(w, fmt):
    k, n = w.shape
    w = f64(np.asarray(w, np.float32).astype(ml_dtypes.bfloat16)).reshape(k // 32, 32, n)
    amax = np.abs(w).max(1)
    if fmt == "e4m3":
        byte = np.frexp(amax)[1] - 1 + 127 - 7
    else:
        mant, ex = np.frexp(amax / 6.0)
        byte = np.where(mant > 0.5, ex, ex - 1) + 127
    byte = np.clip(np.where(amax > 0, byte, 1), 1, 254)
    scaled = (w * np.exp2(127.0 - byte)[:, None, :]).reshape(k, n).astype(np.float32)
    by_word = np.ascontiguousarray(scaled.reshape(k // 512, 128, 4, n).transpose(0, 1, 3, 2))
    if fmt == "e4m3":
        words = by_word.astype(ml_dtypes.float8_e4m3fn).view(np.uint8)
    else:
        c = by_word.astype(ml_dtypes.float4_e2m1fn).view(np.uint8) & 0xF
        words = (c[..., 0::2] | (c[..., 1::2] << 4)).reshape(k // 512, 128, 2 * n)
    return np.ascontiguousarray(words), np.ascontiguousarray(byte.astype(np.uint8).reshape(k // 512, 16, n))


def unpack_weight(words, scales, fmt):
    g, _, n = scales.shape
    words = np.ascontiguousarray(words).reshape(g, 128, n, -1)
    if fmt == "e4m3":
        vals = words.view(ml_dtypes.float8_e4m3fn).astype(np.float64)
    else:
        nib = np.empty((g, 128, n, 4), np.uint8)
        nib[..., 0::2] = words & 0xF
        nib[..., 1::2] = words >> 4
        vals = E2M1[nib]
    vals = vals * np.repeat(np.exp2(scales.astype(np.float64) - 127.0), 8, axis=1)[..., None]
    return vals.transpose(0, 1, 3, 2).reshape(g * 512, n)


K, M, T, S = 1536, 128, 4096, 1536


def setup_inputs():
    n = np.random.standard_normal
    s = mx_kscale(K)[:, None]
    w = n((K, M)) / np.sqrt(K) / s
    v = pack_weight(n((K, T)) * s, "e4m3")
    p_w4 = pack_weight(w[512:], "e2m1")
    return {
        "tab_words": v[0],
        "tab_scales": v[1],
        "w8": (w[:512]).astype(np.float32),
        "w4_words": p_w4[0],
        "w4_scales": p_w4[1],
        "gT": n((M, T)).astype(np.float32),
        "b": (0.3 * n(128)).astype(np.float32),
        "offs": striped(np.random.permutation(T)[:S]),
    }


def reference(tab_words, tab_scales, w8, w4_words, w4_scales, gT, b, offs):
    tab_ = unpack_weight(tab_words, tab_scales, "e4m3")[:, unstriped(offs)]
    w8_ = mxq(f64(w8), 0, "e4m3")
    w4_ = unpack_weight(w4_words, w4_scales, "e2m1")
    y = w8_.T @ tab_[:512] + w4_.T @ tab_[512:]
    return (y + f64(b)[:, None]) * f64(gT)[:, unstriped(offs)]

@@ -1,0 +1,127 @@
+from contextlib import ExitStack
+
+import concourse.mybir as mybir
+
+K, M, T, S = 1536, 128, 4096, 1536
+FLOPS = 2 * K * M * S
+
+F32 = mybir.dt.float32
+BF16 = mybir.dt.bfloat16
+I32 = mybir.dt.int32
+U32 = mybir.dt.uint32
+U16 = mybir.dt.uint16
+U8 = mybir.dt.uint8
+FP8X4 = mybir.dt.float8_e4m3fn_x4
+FP4X4 = mybir.dt.float4_e2m1fn_x4
+IDENT = mybir.ActivationFunctionType.Identity
+MULT = mybir.AluOpType.mult
+
+P = 128
+PACK = 4
+PASSES = 3
+N_TILE = 512
+PER_COL = 16
+GATE_CUTS = (0, 512, 1024, 1280, 1408, 1536)
+
+
+def tile_list_tabgate_bias_kernel(
+    tc, tab_words, tab_scales, w8, w4_words, w4_scales, gT, b, offs, out
+):
+    nc = tc.nc
+    with ExitStack() as ctx:
+        keep = ctx.enter_context(tc.tile_pool(name="keep", bufs=1))
+        psum = ctx.enter_context(tc.psum_pool(name="psum", bufs=1))
+
+        offsets = keep.tile([P, S // PER_COL], U16, name="offsets")
+        scale_win = keep.tile([P, T // 4], I32, name="scale_win", align_bytes=64)
+        word_win = [keep.tile([P, T], I32, name="word_win%d" % a, align_bytes=64) for a in range(PASSES)]
+        gate_win = keep.tile([P, T], F32, name="gate_win", align_bytes=64)
+        w8_raw = keep.tile([P, PACK, M], F32, name="w8_raw", align_bytes=64)
+        w8_bf = keep.tile([P, M, PACK], BF16, name="w8_bf", align_bytes=64)
+        w8_codes = keep.tile([P, M], U32, name="w8_codes", align_bytes=64)
+        w8_scales = keep.tile([P, M], U8, name="w8_scales", align_bytes=64)
+        w4_codes = keep.tile([P, 2, 2 * M], U8, name="w4_codes", align_bytes=64)
+        w4_planes = keep.tile([P, 2, M // 4], I32, name="w4_planes", align_bytes=64)
+        bias = keep.tile([P, 1], F32, name="bias", align_bytes=64)
+        picked_rows = keep.tile([P, S // 4], I32, name="picked_rows", align_bytes=64)
+        planes = [keep.tile([P, S // 4], I32, name="planes%d" % i, align_bytes=64) for i in range(2)]
+        picked = [keep.tile([P, S], U32, name="picked%d" % a, align_bytes=64) for a in range(PASSES)]
+        biased = keep.tile([P, S], F32, name="biased", align_bytes=64)
+        acc = [psum.tile([P, N_TILE], F32, name="acc%d" % s) for s in range(S // N_TILE)]
+
+        scale_rows = tab_scales.rearrange("a q t -> (a q) t").bitcast(I32)
+        words = [tab_words[a].rearrange("p t i -> p (t i)").bitcast(I32) for a in range(PASSES)]
+
+        nc.sync.dma_start(offsets[:], offs)
+        nc.sync.dma_start(scale_win[0:32, :], scale_rows[0:32, :])
+        nc.sync.dma_start(scale_win[64:96, :], scale_rows[16:48, :])
+        nc.sync.dma_start(word_win[0][:], words[0])
+        nc.sync.dma_start(w8_raw[:], w8.rearrange("(p j) n -> p j n", j=PACK))
+        nc.sync.dma_start(word_win[1][:], words[1])
+        nc.sync.dma_start(word_win[2][:], words[2])
+        nc.sync.dma_start(gate_win[:], gT)
+
+        nc.vector.memset(w4_planes[:], 0)
+        nc.vector.memset(scale_win[32:64, :], 0)
+        nc.vector.memset(scale_win[96:128, :], 0)
+        for plane in planes:
+            nc.vector.memset(plane[:], 0)
+
+        nc.gpsimd.dma_start(w4_codes[:].bitcast(I32), w4_words.rearrange("a p n -> p a n").bitcast(I32))
+        w4_rows = w4_scales.bitcast(I32).rearrange("a (q r) n -> r q a n", r=4)
+        for r in range(4):
+            nc.gpsimd.dma_start(w4_planes[r:P:32, :, :], w4_rows[r])
+        with nc.allow_non_contiguous_dma(reason="one bias value a partition"):
+            nc.gpsimd.dma_start(bias[:], b.rearrange("(p o) -> p o", o=1))
+
+        nc.vector.tensor_copy(picked_rows[:].bitcast(U8), scale_win[:].bitcast(U8).indirect(offsets[:]))
+
+        first_row = (0, 16, 80)
+        plane_of = ((0, 4), (0, 0), (1, 0))
+        for a in range(PASSES):
+            i, k = plane_of[a]
+            for r in range(4):
+                queue = nc.scalar if r < 2 else nc.gpsimd
+                queue.dma_start(
+                    planes[i][k + r : P : 32, :], picked_rows[first_row[a] + r : first_row[a] + 16 : 4, :]
+                )
+
+        nc.scalar.activation(w8_bf[:], w8_raw[:].rearrange("p j n -> p n j"), IDENT)
+        nc.vector.tensor_copy(picked[0][:], word_win[0][:].bitcast(U32).indirect(offsets[:]))
+        nc.vector.quantize_mx(
+            out=w8_codes[:].bitcast(FP8X4), scales=w8_scales[:], in_=w8_bf[:].rearrange("p n j -> p (n j)")
+        )
+        nc.vector.tensor_copy(picked[1][:], word_win[1][:].bitcast(U32).indirect(offsets[:]))
+
+        def one_pass(a, s):
+            i, k = plane_of[a]
+            if a == 0:
+                lhsT, lhsT_scale = w8_codes[:].bitcast(FP8X4), w8_scales[:]
+            else:
+                lhsT, lhsT_scale = w4_codes[:, a - 1, :].bitcast(FP4X4), w4_planes[:, a - 1, :].bitcast(U8)
+            nc.tensor.matmul_mx(
+                out=acc[s][:],
+                lhsT=lhsT,
+                lhsT_scale=lhsT_scale,
+                rhs=picked[a][:, s * N_TILE : (s + 1) * N_TILE].bitcast(FP8X4),
+                rhs_scale=planes[i][k:P, s * N_TILE // 4 : (s + 1) * N_TILE // 4].bitcast(U8),
+                start=(a == 0),
+                stop=(a == PASSES - 1),
+            )
+
+        for a in range(PASSES - 1):
+            for s in range(S // N_TILE):
+                one_pass(a, s)
+
+        for s in range(S // N_TILE):
+            cols = slice(s * N_TILE, (s + 1) * N_TILE)
+            entries = offsets[:, cols.start // PER_COL : cols.stop // PER_COL]
+            nc.vector.tensor_copy(picked[2][:, cols], word_win[2][:].bitcast(U32).indirect(entries))
+            one_pass(2, s)
+            nc.scalar.activation(biased[:, cols], acc[s][:], IDENT, bias=bias[:])
+
+        for c0, c1 in zip(GATE_CUTS[:-1], GATE_CUTS[1:]):
+            gated = keep.tile([P, c1 - c0], F32, name="gated%d" % c0, align_bytes=64)
+            entries = offsets[:, c0 // PER_COL : c1 // PER_COL]
+            nc.vector.tensor_tensor(gated[:], gate_win[:].indirect(entries), biased[:, c0:c1], MULT)
+            nc.sync.dma_start(out[:, c0:c1], gated[:])

@@ -53,10 +53,10 @@ def tile_list_tabgate_bias_kernel(
         words = [tab_words[a].rearrange("p t i -> p (t i)").bitcast(I32) for a in range(PASSES)]
 
         nc.sync.dma_start(offsets[:], offs)
-        nc.sync.dma_start(scale_win[0:32, :], scale_rows[0:32, :])
+        nc.sync.dma_start(scale_win[0:32:2, :], scale_rows[16:32, :])
+        nc.sync.dma_start(scale_win[1:32:2, :], scale_rows[0:16, :])
         nc.sync.dma_start(scale_win[64:96, :], scale_rows[16:48, :])
         nc.sync.dma_start(word_win[0][:], words[0])
-        nc.sync.dma_start(w8_raw[:], w8.rearrange("(p j) n -> p j n", j=PACK))
         nc.sync.dma_start(word_win[1][:], words[1])
         nc.sync.dma_start(word_win[2][:], words[2])
         nc.sync.dma_start(gate_win[:], gT)
@@ -64,9 +64,9 @@ def tile_list_tabgate_bias_kernel(
         nc.vector.memset(w4_planes[:], 0)
         nc.vector.memset(scale_win[32:64, :], 0)
         nc.vector.memset(scale_win[96:128, :], 0)
-        for plane in planes:
-            nc.vector.memset(plane[:], 0)
+        nc.vector.memset(planes[1][:], 0)
 
+        nc.gpsimd.dma_start(w8_raw[:], w8.rearrange("(p j) n -> p j n", j=PACK))
         nc.gpsimd.dma_start(w4_codes[:].bitcast(I32), w4_words.rearrange("a p n -> p a n").bitcast(I32))
         w4_rows = w4_scales.bitcast(I32).rearrange("a (q r) n -> r q a n", r=4)
         for r in range(4):
@@ -76,18 +76,15 @@ def tile_list_tabgate_bias_kernel(
 
         nc.vector.tensor_copy(picked_rows[:].bitcast(U8), scale_win[:].bitcast(U8).indirect(offsets[:]))
 
-        first_row = (0, 16, 80)
         plane_of = ((0, 4), (0, 0), (1, 0))
-        for a in range(PASSES):
-            i, k = plane_of[a]
-            for r in range(4):
-                queue = nc.scalar if r < 2 else nc.gpsimd
-                queue.dma_start(
-                    planes[i][k + r : P : 32, :], picked_rows[first_row[a] + r : first_row[a] + 16 : 4, :]
-                )
+        for r in range(4):
+            nc.scalar.dma_start(planes[0][r:P:4, :], picked_rows[2 * r : 2 * r + 32, :])
+        for r in range(4):
+            queue = nc.scalar if r < 2 else nc.gpsimd
+            queue.dma_start(planes[1][r:P:32, :], picked_rows[80 + r : 96 : 4, :])
 
-        nc.scalar.activation(w8_bf[:], w8_raw[:].rearrange("p j n -> p n j"), IDENT)
         nc.vector.tensor_copy(picked[0][:], word_win[0][:].bitcast(U32).indirect(offsets[:]))
+        nc.vector.tensor_copy(w8_bf[:], w8_raw[:].rearrange("p j n -> p n j"))
         nc.vector.quantize_mx(
             out=w8_codes[:].bitcast(FP8X4), scales=w8_scales[:], in_=w8_bf[:].rearrange("p n j -> p (n j)")
         )

@@ -57,6 +57,7 @@ def tile_list_tabgate_bias_kernel(
         nc.sync.dma_start(scale_win[1:32:2, :], scale_rows[0:16, :])
         nc.sync.dma_start(scale_win[64:96, :], scale_rows[16:48, :])
         nc.sync.dma_start(word_win[0][:], words[0])
+        nc.sync.dma_start(w8_raw[:], w8.rearrange("(p j) n -> p j n", j=PACK))
         nc.sync.dma_start(word_win[1][:], words[1])
         nc.sync.dma_start(word_win[2][:], words[2])
         nc.sync.dma_start(gate_win[:], gT)
@@ -66,7 +67,6 @@ def tile_list_tabgate_bias_kernel(
         nc.vector.memset(scale_win[96:128, :], 0)
         nc.vector.memset(planes[1][:], 0)
 
-        nc.gpsimd.dma_start(w8_raw[:], w8.rearrange("(p j) n -> p j n", j=PACK))
         nc.gpsimd.dma_start(w4_codes[:].bitcast(I32), w4_words.rearrange("a p n -> p a n").bitcast(I32))
         w4_rows = w4_scales.bitcast(I32).rearrange("a (q r) n -> r q a n", r=4)
         for r in range(4):
@@ -80,7 +80,7 @@ def tile_list_tabgate_bias_kernel(
         for r in range(4):
             nc.scalar.dma_start(planes[0][r:P:4, :], picked_rows[2 * r : 2 * r + 32, :])
         for r in range(4):
-            queue = nc.scalar if r < 2 else nc.gpsimd
+            queue = nc.scalar if r < 1 else nc.gpsimd
             queue.dma_start(planes[1][r:P:32, :], picked_rows[80 + r : 96 : 4, :])
 
         nc.vector.tensor_copy(picked[0][:], word_win[0][:].bitcast(U32).indirect(offsets[:]))

@@ -33,9 +33,11 @@ def tile_list_tabgate_bias_kernel(
         psum = ctx.enter_context(tc.psum_pool(name="psum", bufs=1))
 
         offsets = keep.tile([P, S // PER_COL], U16, name="offsets")
-        scale_win = keep.tile([P, T // 4], I32, name="scale_win", align_bytes=64)
-        word_win = [keep.tile([P, T], I32, name="word_win%d" % a, align_bytes=64) for a in range(PASSES)]
-        gate_win = keep.tile([P, T], F32, name="gate_win", align_bytes=64)
+        scale_win = keep.tile([P, T // 4], I32, name="scale_win", tag="slot_a", align_bytes=64)
+        word_win = [
+            keep.tile([P, T], I32, name="word_win0", tag="slot_b", align_bytes=64),
+            keep.tile([P, T], I32, name="word_win1", align_bytes=64),
+        ]
         w8_raw = keep.tile([P, PACK, M], F32, name="w8_raw", align_bytes=64)
         w8_bf = keep.tile([P, M, PACK], BF16, name="w8_bf", align_bytes=64)
         w8_codes = keep.tile([P, M], U32, name="w8_codes", align_bytes=64)
@@ -59,8 +61,6 @@ def tile_list_tabgate_bias_kernel(
         nc.sync.dma_start(word_win[0][:], words[0])
         nc.sync.dma_start(w8_raw[:], w8.rearrange("(p j) n -> p j n", j=PACK))
         nc.sync.dma_start(word_win[1][:], words[1])
-        nc.sync.dma_start(word_win[2][:], words[2])
-        nc.sync.dma_start(gate_win[:], gT)
 
         nc.vector.memset(w4_planes[:], 0)
         nc.vector.memset(scale_win[32:64, :], 0)
@@ -78,12 +78,17 @@ def tile_list_tabgate_bias_kernel(
 
         plane_of = ((0, 4), (0, 0), (1, 0))
         for r in range(4):
-            nc.scalar.dma_start(planes[0][r:P:4, :], picked_rows[2 * r : 2 * r + 32, :])
-        for r in range(4):
-            queue = nc.scalar if r < 1 else nc.gpsimd
-            queue.dma_start(planes[1][r:P:32, :], picked_rows[80 + r : 96 : 4, :])
+            nc.sync.dma_start(planes[0][r:P:4, :], picked_rows[2 * r : 2 * r + 32, :])
+        for r in range(2):
+            nc.sync.dma_start(planes[1][r:P:32, :], picked_rows[80 + r : 96 : 4, :])
+        word_win.append(keep.tile([P, T], I32, name="word_win2", tag="slot_a", align_bytes=64))
+        nc.sync.dma_start(word_win[2][:], words[2])
+        for r in range(2, 4):
+            nc.sync.dma_start(planes[1][r:P:32, :], picked_rows[80 + r : 96 : 4, :])
 
         nc.vector.tensor_copy(picked[0][:], word_win[0][:].bitcast(U32).indirect(offsets[:]))
+        gate_win = keep.tile([P, T], F32, name="gate_win", tag="slot_b", align_bytes=64)
+        nc.sync.dma_start(gate_win[:], gT)
         nc.vector.tensor_copy(w8_bf[:], w8_raw[:].rearrange("p j n -> p n j"))
         nc.vector.quantize_mx(
             out=w8_codes[:].bitcast(FP8X4), scales=w8_scales[:], in_=w8_bf[:].rearrange("p n j -> p (n j)")

@@ -89,7 +89,7 @@ def tile_list_tabgate_bias_kernel(
         nc.vector.tensor_copy(picked[0][:], word_win[0][:].bitcast(U32).indirect(offsets[:]))
         gate_win = keep.tile([P, T], F32, name="gate_win", tag="slot_b", align_bytes=64)
         nc.sync.dma_start(gate_win[:], gT)
-        nc.vector.tensor_copy(w8_bf[:], w8_raw[:].rearrange("p j n -> p n j"))
+        nc.scalar.copy(w8_bf[:], w8_raw[:].rearrange("p j n -> p n j"))
         nc.vector.quantize_mx(
             out=w8_codes[:].bitcast(FP8X4), scales=w8_scales[:], in_=w8_bf[:].rearrange("p n j -> p (n j)")
         )

@@ -55,15 +55,15 @@ def tile_list_tabgate_bias_kernel(
         words = [tab_words[a].rearrange("p t i -> p (t i)").bitcast(I32) for a in range(PASSES)]
 
         nc.sync.dma_start(offsets[:], offs)
-        nc.sync.dma_start(scale_win[0:32:2, :], scale_rows[16:32, :])
-        nc.sync.dma_start(scale_win[1:32:2, :], scale_rows[0:16, :])
-        nc.sync.dma_start(scale_win[64:96, :], scale_rows[16:48, :])
+        nc.sync.dma_start(scale_win[64:96:2, :], scale_rows[16:32, :])
+        nc.sync.dma_start(scale_win[48:64, :], scale_rows[32:48, :])
+        nc.sync.dma_start(scale_win[65:96:2, :], scale_rows[0:16, :])
         nc.sync.dma_start(word_win[0][:], words[0])
         nc.sync.dma_start(w8_raw[:], w8.rearrange("(p j) n -> p j n", j=PACK))
         nc.sync.dma_start(word_win[1][:], words[1])
 
         nc.vector.memset(w4_planes[:], 0)
-        nc.vector.memset(scale_win[32:64, :], 0)
+        nc.vector.memset(scale_win[0:48, :], 0)
         nc.vector.memset(scale_win[96:128, :], 0)
         nc.vector.memset(planes[1][:], 0)
 
@@ -78,13 +78,13 @@ def tile_list_tabgate_bias_kernel(
 
         plane_of = ((0, 4), (0, 0), (1, 0))
         for r in range(4):
-            nc.sync.dma_start(planes[0][r:P:4, :], picked_rows[2 * r : 2 * r + 32, :])
+            nc.sync.dma_start(planes[0][r:P:4, :], picked_rows[64 + 2 * r : 96 + 2 * r, :])
         for r in range(2):
-            nc.sync.dma_start(planes[1][r:P:32, :], picked_rows[80 + r : 96 : 4, :])
+            nc.sync.dma_start(planes[1][r:P:32, :], picked_rows[48 + r : 64 : 4, :])
         word_win.append(keep.tile([P, T], I32, name="word_win2", tag="slot_a", align_bytes=64))
         nc.sync.dma_start(word_win[2][:], words[2])
         for r in range(2, 4):
-            nc.sync.dma_start(planes[1][r:P:32, :], picked_rows[80 + r : 96 : 4, :])
+            nc.sync.dma_start(planes[1][r:P:32, :], picked_rows[48 + r : 64 : 4, :])
 
         nc.vector.tensor_copy(picked[0][:], word_win[0][:].bitcast(U32).indirect(offsets[:]))
         gate_win = keep.tile([P, T], F32, name="gate_win", tag="slot_b", align_bytes=64)

@@ -34,38 +34,31 @@ def tile_list_tabgate_bias_kernel(
 
         offsets = keep.tile([P, S // PER_COL], U16, name="offsets")
         scale_win = keep.tile([P, T // 4], I32, name="scale_win", tag="slot_a", align_bytes=64)
-        word_win = [
-            keep.tile([P, T], I32, name="word_win0", tag="slot_b", align_bytes=64),
-            keep.tile([P, T], I32, name="word_win1", align_bytes=64),
-        ]
-        w8_raw = keep.tile([P, PACK, M], F32, name="w8_raw", align_bytes=64)
-        w8_bf = keep.tile([P, M, PACK], BF16, name="w8_bf", align_bytes=64)
+        w8_raw = keep.tile([P, PACK, M], F32, name="w8_raw", tag="slot_b", align_bytes=64)
+        w8_bf = keep.tile([P, M, PACK], BF16, name="w8_bf", tag="slot_c", align_bytes=64)
+        word_win = [keep.tile([P, T], I32, name="word_win0", align_bytes=64)]
         w8_codes = keep.tile([P, M], U32, name="w8_codes", align_bytes=64)
         w8_scales = keep.tile([P, M], U8, name="w8_scales", align_bytes=64)
         w4_codes = keep.tile([P, 2, 2 * M], U8, name="w4_codes", align_bytes=64)
         w4_planes = keep.tile([P, 2, M // 4], I32, name="w4_planes", align_bytes=64)
         bias = keep.tile([P, 1], F32, name="bias", align_bytes=64)
         picked_rows = keep.tile([P, S // 4], I32, name="picked_rows", align_bytes=64)
-        planes = [keep.tile([P, S // 4], I32, name="planes%d" % i, align_bytes=64) for i in range(2)]
+        planes = keep.tile([P, 2, S // 4], I32, name="planes", align_bytes=64)
         picked = [keep.tile([P, S], U32, name="picked%d" % a, align_bytes=64) for a in range(PASSES)]
         biased = keep.tile([P, S], F32, name="biased", align_bytes=64)
         acc = [psum.tile([P, N_TILE], F32, name="acc%d" % s) for s in range(S // N_TILE)]
 
-        scale_rows = tab_scales.rearrange("a q t -> (a q) t").bitcast(I32)
         words = [tab_words[a].rearrange("p t i -> p (t i)").bitcast(I32) for a in range(PASSES)]
 
-        nc.sync.dma_start(offsets[:], offs)
-        nc.sync.dma_start(scale_win[64:96:2, :], scale_rows[16:32, :])
-        nc.sync.dma_start(scale_win[48:64, :], scale_rows[32:48, :])
-        nc.sync.dma_start(scale_win[65:96:2, :], scale_rows[0:16, :])
-        nc.sync.dma_start(word_win[0][:], words[0])
-        nc.sync.dma_start(w8_raw[:], w8.rearrange("(p j) n -> p j n", j=PACK))
-        nc.sync.dma_start(word_win[1][:], words[1])
-
+        nc.vector.memset(scale_win[:], 0)
         nc.vector.memset(w4_planes[:], 0)
-        nc.vector.memset(scale_win[0:48, :], 0)
-        nc.vector.memset(scale_win[96:128, :], 0)
-        nc.vector.memset(planes[1][:], 0)
+
+        nc.sync.dma_start(offsets[:], offs)
+        nc.sync.dma_start(w8_raw[:], w8.rearrange("(p j) n -> p j n", j=PACK))
+        nc.sync.dma_start(word_win[0][:], words[0])
+        place_of = (2, 0, 1)
+        for a in range(PASSES):
+            nc.sync.dma_start(scale_win[32 + place_of[a] : 96 : 4, :], tab_scales[a].bitcast(I32))
 
         nc.gpsimd.dma_start(w4_codes[:].bitcast(I32), w4_words.rearrange("a p n -> p a n").bitcast(I32))
         w4_rows = w4_scales.bitcast(I32).rearrange("a (q r) n -> r q a n", r=4)
@@ -74,26 +67,24 @@ def tile_list_tabgate_bias_kernel(
         with nc.allow_non_contiguous_dma(reason="one bias value a partition"):
             nc.gpsimd.dma_start(bias[:], b.rearrange("(p o) -> p o", o=1))
 
-        nc.vector.tensor_copy(picked_rows[:].bitcast(U8), scale_win[:].bitcast(U8).indirect(offsets[:]))
-
-        plane_of = ((0, 4), (0, 0), (1, 0))
-        for r in range(4):
-            nc.sync.dma_start(planes[0][r:P:4, :], picked_rows[64 + 2 * r : 96 + 2 * r, :])
-        for r in range(2):
-            nc.sync.dma_start(planes[1][r:P:32, :], picked_rows[48 + r : 64 : 4, :])
-        word_win.append(keep.tile([P, T], I32, name="word_win2", tag="slot_a", align_bytes=64))
-        nc.sync.dma_start(word_win[2][:], words[2])
-        for r in range(2, 4):
-            nc.sync.dma_start(planes[1][r:P:32, :], picked_rows[48 + r : 64 : 4, :])
-
-        nc.vector.tensor_copy(picked[0][:], word_win[0][:].bitcast(U32).indirect(offsets[:]))
-        gate_win = keep.tile([P, T], F32, name="gate_win", tag="slot_b", align_bytes=64)
-        nc.sync.dma_start(gate_win[:], gT)
         nc.scalar.copy(w8_bf[:], w8_raw[:].rearrange("p j n -> p n j"))
+        word_win.append(keep.tile([P, T], I32, name="word_win1", tag="slot_b", align_bytes=64))
+        nc.sync.dma_start(word_win[1][:], words[1])
         nc.vector.quantize_mx(
             out=w8_codes[:].bitcast(FP8X4), scales=w8_scales[:], in_=w8_bf[:].rearrange("p n j -> p (n j)")
         )
+        word_win.append(keep.tile([P, T], I32, name="word_win2", tag="slot_c", align_bytes=64))
+        nc.sync.dma_start(word_win[2][:], words[2])
+
+        nc.vector.tensor_copy(picked[0][:], word_win[0][:].bitcast(U32).indirect(offsets[:]))
+        nc.vector.tensor_copy(picked_rows[:].bitcast(U8), scale_win[:].bitcast(U8).indirect(offsets[:]))
+        for r in range(4):
+            nc.sync.dma_start(planes[r:P:4, :, :], picked_rows[32 + 4 * r : 96 + 4 * r, :])
+        gate_win = keep.tile([P, T], F32, name="gate_win", tag="slot_a", align_bytes=64)
+        nc.sync.dma_start(gate_win[:], gT)
         nc.vector.tensor_copy(picked[1][:], word_win[1][:].bitcast(U32).indirect(offsets[:]))
+
+        plane_of = ((0, 4), (0, 0), (1, 0))
 
         def one_pass(a, s):
             i, k = plane_of[a]
@@ -106,7 +97,7 @@ def tile_list_tabgate_bias_kernel(
                 lhsT=lhsT,
                 lhsT_scale=lhsT_scale,
                 rhs=picked[a][:, s * N_TILE : (s + 1) * N_TILE].bitcast(FP8X4),
-                rhs_scale=planes[i][k:P, s * N_TILE // 4 : (s + 1) * N_TILE // 4].bitcast(U8),
+                rhs_scale=planes[k:P, i, s * N_TILE // 4 : (s + 1) * N_TILE // 4].bitcast(U8),
                 start=(a == 0),
                 stop=(a == PASSES - 1),
             )

@@ -21,6 +21,7 @@ PACK = 4
 PASSES = 3
 N_TILE = 512
 PER_COL = 16
+POOL_ZEROS = 384
 GATE_CUTS = (0, 512, 1024, 1280, 1408, 1536)
 
 
@@ -34,9 +35,12 @@ def tile_list_tabgate_bias_kernel(
 
         offsets = keep.tile([P, S // PER_COL], U16, name="offsets")
         scale_win = keep.tile([P, T // 4], I32, name="scale_win", tag="slot_a", align_bytes=64)
-        w8_raw = keep.tile([P, PACK, M], F32, name="w8_raw", tag="slot_b", align_bytes=64)
-        w8_bf = keep.tile([P, M, PACK], BF16, name="w8_bf", tag="slot_c", align_bytes=64)
-        word_win = [keep.tile([P, T], I32, name="word_win0", align_bytes=64)]
+        w8_raw = keep.tile([P, PACK, M], F32, name="w8_raw", align_bytes=64)
+        w8_bf = keep.tile([P, M, PACK], BF16, name="w8_bf", align_bytes=64)
+        word_win = [
+            keep.tile([P, T], I32, name="word_win0", tag="slot_b", align_bytes=64),
+            keep.tile([P, T], I32, name="word_win1", align_bytes=64),
+        ]
         w8_codes = keep.tile([P, M], U32, name="w8_codes", align_bytes=64)
         w8_scales = keep.tile([P, M], U8, name="w8_scales", align_bytes=64)
         w4_codes = keep.tile([P, 2, 2 * M], U8, name="w4_codes", align_bytes=64)
@@ -50,37 +54,38 @@ def tile_list_tabgate_bias_kernel(
 
         words = [tab_words[a].rearrange("p t i -> p (t i)").bitcast(I32) for a in range(PASSES)]
 
-        nc.vector.memset(scale_win[:], 0)
+        nc.gpsimd.memset(scale_win[:, :POOL_ZEROS], 0)
+        nc.vector.memset(scale_win[:, POOL_ZEROS:], 0)
         nc.vector.memset(w4_planes[:], 0)
 
         nc.sync.dma_start(offsets[:], offs)
         nc.sync.dma_start(w8_raw[:], w8.rearrange("(p j) n -> p j n", j=PACK))
-        nc.sync.dma_start(word_win[0][:], words[0])
+        nc.sync.dma_start(w4_codes[:].bitcast(I32), w4_words.rearrange("a p n -> p a n").bitcast(I32))
+        with nc.allow_non_contiguous_dma(reason="one bias value a partition"):
+            nc.sync.dma_start(bias[:], b.rearrange("(p o) -> p o", o=1))
         place_of = (2, 0, 1)
         for a in range(PASSES):
             nc.sync.dma_start(scale_win[32 + place_of[a] : 96 : 4, :], tab_scales[a].bitcast(I32))
+        nc.sync.dma_start(word_win[0][:], words[0])
+        nc.sync.dma_start(word_win[1][:], words[1])
 
-        nc.gpsimd.dma_start(w4_codes[:].bitcast(I32), w4_words.rearrange("a p n -> p a n").bitcast(I32))
         w4_rows = w4_scales.bitcast(I32).rearrange("a (q r) n -> r q a n", r=4)
         for r in range(4):
             nc.gpsimd.dma_start(w4_planes[r:P:32, :, :], w4_rows[r])
-        with nc.allow_non_contiguous_dma(reason="one bias value a partition"):
-            nc.gpsimd.dma_start(bias[:], b.rearrange("(p o) -> p o", o=1))
 
         nc.scalar.copy(w8_bf[:], w8_raw[:].rearrange("p j n -> p n j"))
-        word_win.append(keep.tile([P, T], I32, name="word_win1", tag="slot_b", align_bytes=64))
-        nc.sync.dma_start(word_win[1][:], words[1])
         nc.vector.quantize_mx(
             out=w8_codes[:].bitcast(FP8X4), scales=w8_scales[:], in_=w8_bf[:].rearrange("p n j -> p (n j)")
         )
-        word_win.append(keep.tile([P, T], I32, name="word_win2", tag="slot_c", align_bytes=64))
-        nc.sync.dma_start(word_win[2][:], words[2])
 
-        nc.vector.tensor_copy(picked[0][:], word_win[0][:].bitcast(U32).indirect(offsets[:]))
         nc.vector.tensor_copy(picked_rows[:].bitcast(U8), scale_win[:].bitcast(U8).indirect(offsets[:]))
         for r in range(4):
             nc.sync.dma_start(planes[r:P:4, :, :], picked_rows[32 + 4 * r : 96 + 4 * r, :])
-        gate_win = keep.tile([P, T], F32, name="gate_win", tag="slot_a", align_bytes=64)
+        word_win.append(keep.tile([P, T], I32, name="word_win2", tag="slot_a", align_bytes=64))
+        nc.sync.dma_start(word_win[2][:], words[2])
+
+        nc.vector.tensor_copy(picked[0][:], word_win[0][:].bitcast(U32).indirect(offsets[:]))
+        gate_win = keep.tile([P, T], F32, name="gate_win", tag="slot_b", align_bytes=64)
         nc.sync.dma_start(gate_win[:], gT)
         nc.vector.tensor_copy(picked[1][:], word_win[1][:].bitcast(U32).indirect(offsets[:]))
 

@@ -22,7 +22,7 @@ PASSES = 3
 N_TILE = 512
 PER_COL = 16
 POOL_ZEROS = 384
-GATE_CUTS = (0, 512, 1024, 1280, 1408, 1536)
+GATE_CUTS = (0, 640, 1152, 1408, 1536)
 
 
 def tile_list_tabgate_bias_kernel(
@@ -47,7 +47,7 @@ def tile_list_tabgate_bias_kernel(
         w4_planes = keep.tile([P, 2, M // 4], I32, name="w4_planes", align_bytes=64)
         bias = keep.tile([P, 1], F32, name="bias", align_bytes=64)
         picked_rows = keep.tile([P, S // 4], I32, name="picked_rows", align_bytes=64)
-        planes = keep.tile([P, 2, S // 4], I32, name="planes", align_bytes=64)
+        planes = [keep.tile([P, S // 4], I32, name="planes%d" % i, align_bytes=64) for i in range(2)]
         picked = [keep.tile([P, S], U32, name="picked%d" % a, align_bytes=64) for a in range(PASSES)]
         biased = keep.tile([P, S], F32, name="biased", align_bytes=64)
         acc = [psum.tile([P, N_TILE], F32, name="acc%d" % s) for s in range(S // N_TILE)]
@@ -57,6 +57,7 @@ def tile_list_tabgate_bias_kernel(
         nc.gpsimd.memset(scale_win[:, :POOL_ZEROS], 0)
         nc.vector.memset(scale_win[:, POOL_ZEROS:], 0)
         nc.vector.memset(w4_planes[:], 0)
+        nc.vector.memset(planes[1][:], 0)
 
         nc.sync.dma_start(offsets[:], offs)
         nc.sync.dma_start(w8_raw[:], w8.rearrange("(p j) n -> p j n", j=PACK))
@@ -80,9 +81,13 @@ def tile_list_tabgate_bias_kernel(
 
         nc.vector.tensor_copy(picked_rows[:].bitcast(U8), scale_win[:].bitcast(U8).indirect(offsets[:]))
         for r in range(4):
-            nc.sync.dma_start(planes[r:P:4, :, :], picked_rows[32 + 4 * r : 96 + 4 * r, :])
+            nc.sync.dma_start(planes[0][r:P:4, :], picked_rows[32 + 4 * r : 96 + 4 * r : 2, :])
+        for r in range(2):
+            nc.sync.dma_start(planes[1][r:P:32, :], picked_rows[33 + 4 * r : 96 : 16, :])
         word_win.append(keep.tile([P, T], I32, name="word_win2", tag="slot_a", align_bytes=64))
         nc.sync.dma_start(word_win[2][:], words[2])
+        for r in range(2, 4):
+            nc.sync.dma_start(planes[1][r:P:32, :], picked_rows[33 + 4 * r : 96 : 16, :])
 
         nc.vector.tensor_copy(picked[0][:], word_win[0][:].bitcast(U32).indirect(offsets[:]))
         gate_win = keep.tile([P, T], F32, name="gate_win", tag="slot_b", align_bytes=64)
@@ -102,7 +107,7 @@ def tile_list_tabgate_bias_kernel(
                 lhsT=lhsT,
                 lhsT_scale=lhsT_scale,
                 rhs=picked[a][:, s * N_TILE : (s + 1) * N_TILE].bitcast(FP8X4),
-                rhs_scale=planes[k:P, i, s * N_TILE // 4 : (s + 1) * N_TILE // 4].bitcast(U8),
+                rhs_scale=planes[i][k:P, s * N_TILE // 4 : (s + 1) * N_TILE // 4].bitcast(U8),
                 start=(a == 0),
                 stop=(a == PASSES - 1),
             )

@@ -21,7 +21,7 @@ PACK = 4
 PASSES = 3
 N_TILE = 512
 PER_COL = 16
-POOL_ZEROS = 384
+HEAD_COLS = 1024
 GATE_CUTS = (0, 640, 1152, 1408, 1536)
 
 
@@ -45,7 +45,8 @@ def tile_list_tabgate_bias_kernel(
         w8_scales = keep.tile([P, M], U8, name="w8_scales", align_bytes=64)
         w4_codes = keep.tile([P, 2, 2 * M], U8, name="w4_codes", align_bytes=64)
         w4_planes = keep.tile([P, 2, M // 4], I32, name="w4_planes", align_bytes=64)
-        bias = keep.tile([P, 1], F32, name="bias", align_bytes=64)
+        bias_rows = keep.tile([P, 32], F32, name="bias_rows", align_bytes=64)
+        bias = keep.tile([P, 32], F32, name="bias", align_bytes=64)
         picked_rows = keep.tile([P, S // 4], I32, name="picked_rows", align_bytes=64)
         planes = [keep.tile([P, S // 4], I32, name="planes%d" % i, align_bytes=64) for i in range(2)]
         picked = [keep.tile([P, S], U32, name="picked%d" % a, align_bytes=64) for a in range(PASSES)]
@@ -54,20 +55,20 @@ def tile_list_tabgate_bias_kernel(
 
         words = [tab_words[a].rearrange("p t i -> p (t i)").bitcast(I32) for a in range(PASSES)]
 
-        nc.gpsimd.memset(scale_win[:, :POOL_ZEROS], 0)
-        nc.vector.memset(scale_win[:, POOL_ZEROS:], 0)
-        nc.vector.memset(w4_planes[:], 0)
+        nc.gpsimd.memset(bias_rows[:], 0.0)
+        nc.gpsimd.memset(w4_planes[:], 0)
+        nc.vector.memset(scale_win[:], 0)
         nc.vector.memset(planes[1][:], 0)
 
         nc.sync.dma_start(offsets[:], offs)
+        nc.sync.dma_start(word_win[0][:, :HEAD_COLS], words[0][:, :HEAD_COLS])
         nc.sync.dma_start(w8_raw[:], w8.rearrange("(p j) n -> p j n", j=PACK))
         nc.sync.dma_start(w4_codes[:].bitcast(I32), w4_words.rearrange("a p n -> p a n").bitcast(I32))
-        with nc.allow_non_contiguous_dma(reason="one bias value a partition"):
-            nc.sync.dma_start(bias[:], b.rearrange("(p o) -> p o", o=1))
+        nc.sync.dma_start(bias_rows[0:P:32, :], b.rearrange("(q i) -> q i", i=32))
         place_of = (2, 0, 1)
         for a in range(PASSES):
             nc.sync.dma_start(scale_win[32 + place_of[a] : 96 : 4, :], tab_scales[a].bitcast(I32))
-        nc.sync.dma_start(word_win[0][:], words[0])
+        nc.sync.dma_start(word_win[0][:, HEAD_COLS:], words[0][:, HEAD_COLS:])
         nc.sync.dma_start(word_win[1][:], words[1])
 
         w4_rows = w4_scales.bitcast(I32).rearrange("a (q r) n -> r q a n", r=4)
@@ -79,6 +80,7 @@ def tile_list_tabgate_bias_kernel(
             out=w8_codes[:].bitcast(FP8X4), scales=w8_scales[:], in_=w8_bf[:].rearrange("p n j -> p (n j)")
         )
 
+        nc.vector.transpose(bias[:], bias_rows[:])
         nc.vector.tensor_copy(picked_rows[:].bitcast(U8), scale_win[:].bitcast(U8).indirect(offsets[:]))
         for r in range(4):
             nc.sync.dma_start(planes[0][r:P:4, :], picked_rows[32 + 4 * r : 96 + 4 * r : 2, :])
@@ -121,7 +123,7 @@ def tile_list_tabgate_bias_kernel(
             entries = offsets[:, cols.start // PER_COL : cols.stop // PER_COL]
             nc.vector.tensor_copy(picked[2][:, cols], word_win[2][:].bitcast(U32).indirect(entries))
             one_pass(2, s)
-            nc.scalar.activation(biased[:, cols], acc[s][:], IDENT, bias=bias[:])
+            nc.scalar.activation(biased[:, cols], acc[s][:], IDENT, bias=bias[:, 0:1])
 
         for c0, c1 in zip(GATE_CUTS[:-1], GATE_CUTS[1:]):
             gated = keep.tile([P, c1 - c0], F32, name="gated%d" % c0, align_bytes=64)

@@ -22,7 +22,7 @@ PASSES = 3
 N_TILE = 512
 PER_COL = 16
 HEAD_COLS = 1024
-GATE_CUTS = (0, 640, 1152, 1408, 1536)
+GATE_CUTS = (0, 800, 1216, 1408, 1536)
 
 
 def tile_list_tabgate_bias_kernel(

@@ -22,7 +22,9 @@ PASSES = 3
 N_TILE = 512
 PER_COL = 16
 HEAD_COLS = 1024
-GATE_CUTS = (0, 800, 1216, 1408, 1536)
+EARLY = 896
+N_LATE = 128
+GATE_CUTS = (0, EARLY, 1152, 1408, 1536)
 
 
 def tile_list_tabgate_bias_kernel(
@@ -39,7 +41,7 @@ def tile_list_tabgate_bias_kernel(
         w8_bf = keep.tile([P, M, PACK], BF16, name="w8_bf", align_bytes=64)
         word_win = [
             keep.tile([P, T], I32, name="word_win0", tag="slot_b", align_bytes=64),
-            keep.tile([P, T], I32, name="word_win1", align_bytes=64),
+            keep.tile([P, T], I32, name="word_win1", tag="slot_c", align_bytes=64),
         ]
         w8_codes = keep.tile([P, M], U32, name="w8_codes", align_bytes=64)
         w8_scales = keep.tile([P, M], U8, name="w8_scales", align_bytes=64)
@@ -48,17 +50,19 @@ def tile_list_tabgate_bias_kernel(
         bias_rows = keep.tile([P, 32], F32, name="bias_rows", align_bytes=64)
         bias = keep.tile([P, 32], F32, name="bias", align_bytes=64)
         picked_rows = keep.tile([P, S // 4], I32, name="picked_rows", align_bytes=64)
-        planes = [keep.tile([P, S // 4], I32, name="planes%d" % i, align_bytes=64) for i in range(2)]
+        early_planes = keep.tile([P, EARLY // 4], I32, name="early_planes", align_bytes=64)
+        last_plane = keep.tile([P, S // 4], I32, name="last_plane", align_bytes=64)
         picked = [keep.tile([P, S], U32, name="picked%d" % a, align_bytes=64) for a in range(PASSES)]
         biased = keep.tile([P, S], F32, name="biased", align_bytes=64)
-        acc = [psum.tile([P, N_TILE], F32, name="acc%d" % s) for s in range(S // N_TILE)]
+        banks = [(0, N_TILE), (N_TILE, EARLY)] + [(c, c + N_LATE) for c in range(EARLY, S, N_LATE)]
+        acc = [psum.tile([P, N_TILE], F32, name="acc%d" % i) for i in range(len(banks))]
 
         words = [tab_words[a].rearrange("p t i -> p (t i)").bitcast(I32) for a in range(PASSES)]
 
         nc.gpsimd.memset(bias_rows[:], 0.0)
         nc.gpsimd.memset(w4_planes[:], 0)
         nc.vector.memset(scale_win[:], 0)
-        nc.vector.memset(planes[1][:], 0)
+        nc.vector.memset(last_plane[:], 0)
 
         nc.sync.dma_start(offsets[:], offs)
         nc.sync.dma_start(word_win[0][:, :HEAD_COLS], words[0][:, :HEAD_COLS])
@@ -69,11 +73,10 @@ def tile_list_tabgate_bias_kernel(
         for a in range(PASSES):
             nc.sync.dma_start(scale_win[32 + place_of[a] : 96 : 4, :], tab_scales[a].bitcast(I32))
         nc.sync.dma_start(word_win[0][:, HEAD_COLS:], words[0][:, HEAD_COLS:])
-        nc.sync.dma_start(word_win[1][:], words[1])
-
         w4_rows = w4_scales.bitcast(I32).rearrange("a (q r) n -> r q a n", r=4)
         for r in range(4):
-            nc.gpsimd.dma_start(w4_planes[r:P:32, :, :], w4_rows[r])
+            nc.sync.dma_start(w4_planes[r:P:32, :, :], w4_rows[r])
+        nc.sync.dma_start(word_win[1][:], words[1])
 
         nc.scalar.copy(w8_bf[:], w8_raw[:].rearrange("p j n -> p n j"))
         nc.vector.quantize_mx(
@@ -83,47 +86,72 @@ def tile_list_tabgate_bias_kernel(
         nc.vector.transpose(bias[:], bias_rows[:])
         nc.vector.tensor_copy(picked_rows[:].bitcast(U8), scale_win[:].bitcast(U8).indirect(offsets[:]))
         for r in range(4):
-            nc.sync.dma_start(planes[0][r:P:4, :], picked_rows[32 + 4 * r : 96 + 4 * r : 2, :])
+            nc.sync.dma_start(early_planes[r:P:4, :], picked_rows[32 + 4 * r : 96 + 4 * r : 2, : EARLY // 4])
         for r in range(2):
-            nc.sync.dma_start(planes[1][r:P:32, :], picked_rows[33 + 4 * r : 96 : 16, :])
+            nc.sync.dma_start(last_plane[r:P:32, :], picked_rows[33 + 4 * r : 96 : 16, :])
         word_win.append(keep.tile([P, T], I32, name="word_win2", tag="slot_a", align_bytes=64))
         nc.sync.dma_start(word_win[2][:], words[2])
         for r in range(2, 4):
-            nc.sync.dma_start(planes[1][r:P:32, :], picked_rows[33 + 4 * r : 96 : 16, :])
+            nc.sync.dma_start(last_plane[r:P:32, :], picked_rows[33 + 4 * r : 96 : 16, :])
 
         nc.vector.tensor_copy(picked[0][:], word_win[0][:].bitcast(U32).indirect(offsets[:]))
         gate_win = keep.tile([P, T], F32, name="gate_win", tag="slot_b", align_bytes=64)
         nc.sync.dma_start(gate_win[:], gT)
         nc.vector.tensor_copy(picked[1][:], word_win[1][:].bitcast(U32).indirect(offsets[:]))
 
-        plane_of = ((0, 4), (0, 0), (1, 0))
+        late_planes = keep.tile([P, (S - EARLY) // 4], I32, name="late_planes", tag="slot_c", align_bytes=64)
+        for r in range(4):
+            nc.sync.dma_start(late_planes[r:P:4, :], picked_rows[32 + 4 * r : 96 + 4 * r : 2, EARLY // 4 :])
 
-        def one_pass(a, s):
-            i, k = plane_of[a]
+        def passes(a, i, first, last):
+            b0, b1 = banks[i]
+            width = N_TILE if b1 - b0 == N_TILE else N_LATE
             if a == 0:
                 lhsT, lhsT_scale = w8_codes[:].bitcast(FP8X4), w8_scales[:]
             else:
                 lhsT, lhsT_scale = w4_codes[:, a - 1, :].bitcast(FP4X4), w4_planes[:, a - 1, :].bitcast(U8)
-            nc.tensor.matmul_mx(
-                out=acc[s][:],
-                lhsT=lhsT,
-                lhsT_scale=lhsT_scale,
-                rhs=picked[a][:, s * N_TILE : (s + 1) * N_TILE].bitcast(FP8X4),
-                rhs_scale=planes[i][k:P, s * N_TILE // 4 : (s + 1) * N_TILE // 4].bitcast(U8),
-                start=(a == 0),
-                stop=(a == PASSES - 1),
-            )
+            for c0 in range(b0, b1, width):
+                c1 = c0 + width
+                if a == 2:
+                    plane = last_plane[:, c0 // 4 : c1 // 4]
+                else:
+                    k = 4 if a == 0 else 0
+                    if c0 < EARLY:
+                        plane = early_planes[k:P, c0 // 4 : c1 // 4]
+                    else:
+                        plane = late_planes[k:P, (c0 - EARLY) // 4 : (c1 - EARLY) // 4]
+                nc.tensor.matmul_mx(
+                    out=acc[i][:, c0 - b0 : c1 - b0],
+                    lhsT=lhsT,
+                    lhsT_scale=lhsT_scale,
+                    rhs=picked[a][:, c0:c1].bitcast(FP8X4),
+                    rhs_scale=plane.bitcast(U8),
+                    start=(first and c0 == b0),
+                    stop=(last and c1 == b1),
+                )
 
-        for a in range(PASSES - 1):
-            for s in range(S // N_TILE):
-                one_pass(a, s)
+        def add_bias(i):
+            b0, b1 = banks[i]
+            nc.scalar.activation(biased[:, b0:b1], acc[i][:, : b1 - b0], IDENT, bias=bias[:, 0:1])
 
-        for s in range(S // N_TILE):
-            cols = slice(s * N_TILE, (s + 1) * N_TILE)
-            entries = offsets[:, cols.start // PER_COL : cols.stop // PER_COL]
-            nc.vector.tensor_copy(picked[2][:, cols], word_win[2][:].bitcast(U32).indirect(entries))
-            one_pass(2, s)
-            nc.scalar.activation(biased[:, cols], acc[s][:], IDENT, bias=bias[:, 0:1])
+        def pick_last_words(c0, c1):
+            entries = offsets[:, c0 // PER_COL : c1 // PER_COL]
+            nc.vector.tensor_copy(picked[2][:, c0:c1], word_win[2][:].bitcast(U32).indirect(entries))
+
+        for a in range(2):
+            for i in range(2):
+                passes(a, i, a == 0, False)
+        pick_last_words(0, EARLY)
+        for i in range(2):
+            passes(2, i, False, True)
+            add_bias(i)
+        pick_last_words(EARLY, S)
+        for i in range(2, len(banks)):
+            passes(2, i, True, False)
+        for i in range(2, len(banks)):
+            passes(0, i, False, False)
+            passes(1, i, False, True)
+            add_bias(i)
 
         for c0, c1 in zip(GATE_CUTS[:-1], GATE_CUTS[1:]):
             gated = keep.tile([P, c1 - c0], F32, name="gated%d" % c0, align_bytes=64)

@@ -51,7 +51,7 @@ def tile_list_tabgate_bias_kernel(
         bias = keep.tile([P, 32], F32, name="bias", align_bytes=64)
         picked_rows = keep.tile([P, S // 4], I32, name="picked_rows", align_bytes=64)
         early_planes = keep.tile([P, EARLY // 4], I32, name="early_planes", align_bytes=64)
-        last_plane = keep.tile([P, S // 4], I32, name="last_plane", align_bytes=64)
+        last_plane = keep.tile([P, EARLY // 4], I32, name="last_plane", align_bytes=64)
         picked = [keep.tile([P, S], U32, name="picked%d" % a, align_bytes=64) for a in range(PASSES)]
         biased = keep.tile([P, S], F32, name="biased", align_bytes=64)
         banks = [(0, N_TILE), (N_TILE, EARLY)] + [(c, c + N_LATE) for c in range(EARLY, S, N_LATE)]
@@ -88,20 +88,20 @@ def tile_list_tabgate_bias_kernel(
         for r in range(4):
             nc.sync.dma_start(early_planes[r:P:4, :], picked_rows[32 + 4 * r : 96 + 4 * r : 2, : EARLY // 4])
         for r in range(2):
-            nc.sync.dma_start(last_plane[r:P:32, :], picked_rows[33 + 4 * r : 96 : 16, :])
+            nc.sync.dma_start(last_plane[r:P:32, :], picked_rows[33 + 4 * r : 96 : 16, : EARLY // 4])
         word_win.append(keep.tile([P, T], I32, name="word_win2", tag="slot_a", align_bytes=64))
         nc.sync.dma_start(word_win[2][:], words[2])
         for r in range(2, 4):
-            nc.sync.dma_start(last_plane[r:P:32, :], picked_rows[33 + 4 * r : 96 : 16, :])
+            nc.sync.dma_start(last_plane[r:P:32, :], picked_rows[33 + 4 * r : 96 : 16, : EARLY // 4])
 
         nc.vector.tensor_copy(picked[0][:], word_win[0][:].bitcast(U32).indirect(offsets[:]))
         gate_win = keep.tile([P, T], F32, name="gate_win", tag="slot_b", align_bytes=64)
         nc.sync.dma_start(gate_win[:], gT)
         nc.vector.tensor_copy(picked[1][:], word_win[1][:].bitcast(U32).indirect(offsets[:]))
 
-        late_planes = keep.tile([P, (S - EARLY) // 4], I32, name="late_planes", tag="slot_c", align_bytes=64)
+        late_planes = keep.tile([P, 2, (S - EARLY) // 4], I32, name="late_planes", tag="slot_c", align_bytes=64)
         for r in range(4):
-            nc.sync.dma_start(late_planes[r:P:4, :], picked_rows[32 + 4 * r : 96 + 4 * r : 2, EARLY // 4 :])
+            nc.sync.dma_start(late_planes[r:P:4, :, :], picked_rows[32 + 4 * r : 96 + 4 * r, EARLY // 4 :])
 
         def passes(a, i, first, last):
             b0, b1 = banks[i]
@@ -112,14 +112,13 @@ def tile_list_tabgate_bias_kernel(
                 lhsT, lhsT_scale = w4_codes[:, a - 1, :].bitcast(FP4X4), w4_planes[:, a - 1, :].bitcast(U8)
             for c0 in range(b0, b1, width):
                 c1 = c0 + width
-                if a == 2:
+                k = 4 if a == 0 else 0
+                if c0 >= EARLY:
+                    plane = late_planes[k:P, a // 2, (c0 - EARLY) // 4 : (c1 - EARLY) // 4]
+                elif a == 2:
                     plane = last_plane[:, c0 // 4 : c1 // 4]
                 else:
-                    k = 4 if a == 0 else 0
-                    if c0 < EARLY:
-                        plane = early_planes[k:P, c0 // 4 : c1 // 4]
-                    else:
-                        plane = late_planes[k:P, (c0 - EARLY) // 4 : (c1 - EARLY) // 4]
+                    plane = early_planes[k:P, c0 // 4 : c1 // 4]
                 nc.tensor.matmul_mx(
                     out=acc[i][:, c0 - b0 : c1 - b0],
                     lhsT=lhsT,
@@ -147,10 +146,8 @@ def tile_list_tabgate_bias_kernel(
             add_bias(i)
         pick_last_words(EARLY, S)
         for i in range(2, len(banks)):
-            passes(2, i, True, False)
-        for i in range(2, len(banks)):
-            passes(0, i, False, False)
-            passes(1, i, False, True)
+            for a in range(PASSES):
+                passes(a, i, a == 0, a == PASSES - 1)
             add_bias(i)
 
         for c0, c1 in zip(GATE_CUTS[:-1], GATE_CUTS[1:]):

@@ -137,14 +137,17 @@ def tile_list_tabgate_bias_kernel(
             entries = offsets[:, c0 // PER_COL : c1 // PER_COL]
             nc.vector.tensor_copy(picked[2][:, c0:c1], word_win[2][:].bitcast(U32).indirect(entries))
 
-        for a in range(2):
-            for i in range(2):
-                passes(a, i, a == 0, False)
-        pick_last_words(0, EARLY)
-        for i in range(2):
-            passes(2, i, False, True)
-            add_bias(i)
-        pick_last_words(EARLY, S)
+        passes(0, 0, True, False)
+        passes(0, 1, True, False)
+        passes(1, 1, False, False)
+        pick_last_words(0, N_TILE)
+        passes(2, 0, False, False)
+        passes(1, 0, False, True)
+        add_bias(0)
+        pick_last_words(N_TILE, 2 * N_TILE)
+        passes(2, 1, False, True)
+        add_bias(1)
+        pick_last_words(2 * N_TILE, S)
         for i in range(2, len(banks)):
             for a in range(PASSES):
                 passes(a, i, a == 0, a == PASSES - 1)

@@ -22,9 +22,10 @@ PASSES = 3
 N_TILE = 512
 PER_COL = 16
 HEAD_COLS = 1024
-EARLY = 896
+EARLY = 1024
 N_LATE = 128
-GATE_CUTS = (0, EARLY, 1152, 1408, 1536)
+FIRST = 768
+GATE_CUTS = (0, FIRST, 1152, 1408, 1536)
 
 
 def tile_list_tabgate_bias_kernel(
@@ -54,7 +55,7 @@ def tile_list_tabgate_bias_kernel(
         last_plane = keep.tile([P, EARLY // 4], I32, name="last_plane", align_bytes=64)
         picked = [keep.tile([P, S], U32, name="picked%d" % a, align_bytes=64) for a in range(PASSES)]
         biased = keep.tile([P, S], F32, name="biased", align_bytes=64)
-        banks = [(0, N_TILE), (N_TILE, EARLY)] + [(c, c + N_LATE) for c in range(EARLY, S, N_LATE)]
+        banks = [(0, N_TILE), (N_TILE, FIRST), (FIRST, EARLY)] + [(c, c + N_LATE) for c in range(EARLY, S, N_LATE)]
         acc = [psum.tile([P, N_TILE], F32, name="acc%d" % i) for i in range(len(banks))]
 
         words = [tab_words[a].rearrange("p t i -> p (t i)").bitcast(I32) for a in range(PASSES)]
@@ -144,13 +145,13 @@ def tile_list_tabgate_bias_kernel(
         passes(2, 0, False, False)
         passes(1, 0, False, True)
         add_bias(0)
-        pick_last_words(N_TILE, 2 * N_TILE)
+        pick_last_words(N_TILE, EARLY)
         passes(2, 1, False, True)
         add_bias(1)
-        pick_last_words(2 * N_TILE, S)
+        pick_last_words(EARLY, S)
         for i in range(2, len(banks)):
-            for a in range(PASSES):
-                passes(a, i, a == 0, a == PASSES - 1)
+            for a in (2, 0, 1):
+                passes(a, i, a == 2, a == 1)
             add_bias(i)
 
         for c0, c1 in zip(GATE_CUTS[:-1], GATE_CUTS[1:]):

@@ -22,7 +22,7 @@ PASSES = 3
 N_TILE = 512
 PER_COL = 16
 HEAD_COLS = 1024
-EARLY = 1024
+EARLY = 896
 N_LATE = 128
 FIRST = 768
 GATE_CUTS = (0, FIRST, 1152, 1408, 1536)
@@ -56,7 +56,7 @@ def tile_list_tabgate_bias_kernel(
         picked = [keep.tile([P, S], U32, name="picked%d" % a, align_bytes=64) for a in range(PASSES)]
         biased = keep.tile([P, S], F32, name="biased", align_bytes=64)
         banks = [(0, N_TILE), (N_TILE, FIRST), (FIRST, EARLY)] + [(c, c + N_LATE) for c in range(EARLY, S, N_LATE)]
-        acc = [psum.tile([P, N_TILE], F32, name="acc%d" % i) for i in range(len(banks))]
+        acc = [psum.tile([P, N_TILE], F32, name="acc%d" % i) for i in range(2)]
 
         words = [tab_words[a].rearrange("p t i -> p (t i)").bitcast(I32) for a in range(PASSES)]
 
@@ -140,16 +140,17 @@ def tile_list_tabgate_bias_kernel(
 
         passes(0, 0, True, False)
         passes(0, 1, True, False)
-        passes(1, 1, False, False)
         pick_last_words(0, N_TILE)
         passes(2, 0, False, False)
         passes(1, 0, False, True)
         add_bias(0)
-        pick_last_words(N_TILE, EARLY)
-        passes(2, 1, False, True)
+        pick_last_words(N_TILE, 2 * N_TILE)
+        passes(2, 1, False, False)
+        passes(1, 1, False, True)
         add_bias(1)
-        pick_last_words(EARLY, S)
+        pick_last_words(2 * N_TILE, S)
         for i in range(2, len(banks)):
+            acc.append(psum.tile([P, N_TILE], F32, name="acc%d" % i, tag="acc%d" % (1 if i == 2 else i)))
             for a in (2, 0, 1):
                 passes(a, i, a == 2, a == 1)
             add_bias(i)

@@ -88,11 +88,9 @@ def tile_list_tabgate_bias_kernel(
         nc.vector.tensor_copy(picked_rows[:].bitcast(U8), scale_win[:].bitcast(U8).indirect(offsets[:]))
         for r in range(4):
             nc.sync.dma_start(early_planes[r:P:4, :], picked_rows[32 + 4 * r : 96 + 4 * r : 2, : EARLY // 4])
-        for r in range(2):
-            nc.sync.dma_start(last_plane[r:P:32, :], picked_rows[33 + 4 * r : 96 : 16, : EARLY // 4])
         word_win.append(keep.tile([P, T], I32, name="word_win2", tag="slot_a", align_bytes=64))
         nc.sync.dma_start(word_win[2][:], words[2])
-        for r in range(2, 4):
+        for r in range(4):
             nc.sync.dma_start(last_plane[r:P:32, :], picked_rows[33 + 4 * r : 96 : 16, : EARLY // 4])
 
         nc.vector.tensor_copy(picked[0][:], word_win[0][:].bitcast(U32).indirect(offsets[:]))

@@ -21,7 +21,6 @@ PACK = 4
 PASSES = 3
 N_TILE = 512
 PER_COL = 16
-HEAD_COLS = 1024
 EARLY = 896
 N_LATE = 128
 FIRST = 768
@@ -65,17 +64,19 @@ def tile_list_tabgate_bias_kernel(
         nc.vector.memset(scale_win[:], 0)
         nc.vector.memset(last_plane[:], 0)
 
+        w4_rows = w4_scales.bitcast(I32).rearrange("a (q r) n -> r q a n", r=4)
         nc.sync.dma_start(offsets[:], offs)
-        nc.sync.dma_start(word_win[0][:, :HEAD_COLS], words[0][:, :HEAD_COLS])
-        nc.sync.dma_start(w8_raw[:], w8.rearrange("(p j) n -> p j n", j=PACK))
-        nc.sync.dma_start(w4_codes[:].bitcast(I32), w4_words.rearrange("a p n -> p a n").bitcast(I32))
+        nc.sync.dma_start(word_win[0][0:P:2, :], words[0][0:P:2, :])
         nc.sync.dma_start(bias_rows[0:P:32, :], b.rearrange("(q i) -> q i", i=32))
+        for r in range(2):
+            nc.sync.dma_start(w4_planes[r:P:32, :, :], w4_rows[r])
         place_of = (2, 0, 1)
         for a in range(PASSES):
             nc.sync.dma_start(scale_win[32 + place_of[a] : 96 : 4, :], tab_scales[a].bitcast(I32))
-        nc.sync.dma_start(word_win[0][:, HEAD_COLS:], words[0][:, HEAD_COLS:])
-        w4_rows = w4_scales.bitcast(I32).rearrange("a (q r) n -> r q a n", r=4)
-        for r in range(4):
+        nc.sync.dma_start(word_win[0][1:P:2, :], words[0][1:P:2, :])
+        nc.sync.dma_start(w8_raw[:], w8.rearrange("(p j) n -> p j n", j=PACK))
+        nc.sync.dma_start(w4_codes[:].bitcast(I32), w4_words.rearrange("a p n -> p a n").bitcast(I32))
+        for r in range(2, 4):
             nc.sync.dma_start(w4_planes[r:P:32, :, :], w4_rows[r])
         nc.sync.dma_start(word_win[1][:], words[1])
 

@@ -33,10 +33,11 @@ def tile_list_tabgate_bias_kernel(
     nc = tc.nc
     with ExitStack() as ctx:
         keep = ctx.enter_context(tc.tile_pool(name="keep", bufs=1))
+        shared = ctx.enter_context(tc.tile_pool(name="shared", bufs=1))
         psum = ctx.enter_context(tc.psum_pool(name="psum", bufs=1))
 
         offsets = keep.tile([P, S // PER_COL], U16, name="offsets")
-        scale_win = keep.tile([P, T // 4], I32, name="scale_win", tag="slot_a", align_bytes=64)
+        scale_win = shared.tile([P, T // 4], I32, name="scale_win", offset=4 * T - 1024, align_bytes=64)
         w8_raw = keep.tile([P, PACK, M], F32, name="w8_raw", align_bytes=64)
         w8_bf = keep.tile([P, M, PACK], BF16, name="w8_bf", align_bytes=64)
         word_win = [
@@ -45,7 +46,6 @@ def tile_list_tabgate_bias_kernel(
         ]
         w8_codes = keep.tile([P, M], U32, name="w8_codes", align_bytes=64)
         w8_scales = keep.tile([P, M], U8, name="w8_scales", align_bytes=64)
-        w4_codes = keep.tile([P, 2, 2 * M], U8, name="w4_codes", align_bytes=64)
         w4_planes = keep.tile([P, 2, M // 4], I32, name="w4_planes", align_bytes=64)
         bias_rows = keep.tile([P, 32], F32, name="bias_rows", align_bytes=64)
         bias = keep.tile([P, 32], F32, name="bias", align_bytes=64)
@@ -75,7 +75,6 @@ def tile_list_tabgate_bias_kernel(
             nc.sync.dma_start(scale_win[32 + place_of[a] : 96 : 4, :], tab_scales[a].bitcast(I32))
         nc.sync.dma_start(word_win[0][1:P:2, :], words[0][1:P:2, :])
         nc.sync.dma_start(w8_raw[:], w8.rearrange("(p j) n -> p j n", j=PACK))
-        nc.sync.dma_start(w4_codes[:].bitcast(I32), w4_words.rearrange("a p n -> p a n").bitcast(I32))
         for r in range(2, 4):
             nc.sync.dma_start(w4_planes[r:P:32, :, :], w4_rows[r])
         nc.sync.dma_start(word_win[1][:], words[1])
@@ -87,12 +86,14 @@ def tile_list_tabgate_bias_kernel(
 
         nc.vector.transpose(bias[:], bias_rows[:])
         nc.vector.tensor_copy(picked_rows[:].bitcast(U8), scale_win[:].bitcast(U8).indirect(offsets[:]))
-        for r in range(4):
-            nc.sync.dma_start(early_planes[r:P:4, :], picked_rows[32 + 4 * r : 96 + 4 * r : 2, : EARLY // 4])
-        word_win.append(keep.tile([P, T], I32, name="word_win2", tag="slot_a", align_bytes=64))
-        nc.sync.dma_start(word_win[2][:], words[2])
+        word_win.append(shared.tile([P, T], I32, name="word_win2", offset=0, align_bytes=64))
+        w4_codes = shared.tile([P, 2, 2 * M], U8, name="w4_codes", offset=4 * T, align_bytes=64)
         for r in range(4):
             nc.sync.dma_start(last_plane[r:P:32, :], picked_rows[33 + 4 * r : 96 : 16, : EARLY // 4])
+        nc.sync.dma_start(word_win[2][:], words[2])
+        nc.sync.dma_start(w4_codes[:].bitcast(I32), w4_words.rearrange("a p n -> p a n").bitcast(I32))
+        for r in range(4):
+            nc.sync.dma_start(early_planes[r:P:4, :], picked_rows[32 + 4 * r : 96 + 4 * r : 2, : EARLY // 4])
 
         nc.vector.tensor_copy(picked[0][:], word_win[0][:].bitcast(U32).indirect(offsets[:]))
         gate_win = keep.tile([P, T], F32, name="gate_win", tag="slot_b", align_bytes=64)
@@ -137,21 +138,14 @@ def tile_list_tabgate_bias_kernel(
             entries = offsets[:, c0 // PER_COL : c1 // PER_COL]
             nc.vector.tensor_copy(picked[2][:, c0:c1], word_win[2][:].bitcast(U32).indirect(entries))
 
-        passes(0, 0, True, False)
-        passes(0, 1, True, False)
-        pick_last_words(0, N_TILE)
-        passes(2, 0, False, False)
-        passes(1, 0, False, True)
-        add_bias(0)
-        pick_last_words(N_TILE, 2 * N_TILE)
-        passes(2, 1, False, False)
-        passes(1, 1, False, True)
-        add_bias(1)
-        pick_last_words(2 * N_TILE, S)
-        for i in range(2, len(banks)):
-            acc.append(psum.tile([P, N_TILE], F32, name="acc%d" % i, tag="acc%d" % (1 if i == 2 else i)))
-            for a in (2, 0, 1):
-                passes(a, i, a == 2, a == 1)
+        for c0 in range(0, S, N_TILE):
+            pick_last_words(c0, c0 + N_TILE)
+        for i in range(len(banks)):
+            if i >= 2:
+                acc.append(psum.tile([P, N_TILE], F32, name="acc%d" % i, tag="acc%d" % (1 if i == 2 else i)))
+            order = (0, 2, 1) if i < 2 else (2, 0, 1)
+            for a in order:
+                passes(a, i, a == order[0], a == order[-1])
             add_bias(i)
 
         for c0, c1 in zip(GATE_CUTS[:-1], GATE_CUTS[1:]):

@@ -21,10 +21,10 @@ PACK = 4
 PASSES = 3
 N_TILE = 512
 PER_COL = 16
-EARLY = 896
+EARLY = 1024
 N_LATE = 128
 FIRST = 768
-GATE_CUTS = (0, FIRST, 1152, 1408, 1536)
+GATE_CUTS = (0, FIRST, 1280, 1536)
 
 
 def tile_list_tabgate_bias_kernel(
@@ -55,7 +55,7 @@ def tile_list_tabgate_bias_kernel(
         picked = [keep.tile([P, S], U32, name="picked%d" % a, align_bytes=64) for a in range(PASSES)]
         biased = keep.tile([P, S], F32, name="biased", align_bytes=64)
         banks = [(0, N_TILE), (N_TILE, FIRST), (FIRST, EARLY)] + [(c, c + N_LATE) for c in range(EARLY, S, N_LATE)]
-        acc = [psum.tile([P, N_TILE], F32, name="acc%d" % i) for i in range(2)]
+        acc = [psum.tile([P, N_TILE], F32, name="acc%d" % i) for i in range(len(banks))]
 
         words = [tab_words[a].rearrange("p t i -> p (t i)").bitcast(I32) for a in range(PASSES)]
 
@@ -141,9 +141,7 @@ def tile_list_tabgate_bias_kernel(
         for c0 in range(0, S, N_TILE):
             pick_last_words(c0, c0 + N_TILE)
         for i in range(len(banks)):
-            if i >= 2:
-                acc.append(psum.tile([P, N_TILE], F32, name="acc%d" % i, tag="acc%d" % (1 if i == 2 else i)))
-            order = (0, 2, 1) if i < 2 else (2, 0, 1)
+            order = (0, 2, 1) if i < 3 else (2, 0, 1)
             for a in order:
                 passes(a, i, a == order[0], a == order[-1])
             add_bias(i)
@@ -152,4 +150,7 @@ def tile_list_tabgate_bias_kernel(
             gated = keep.tile([P, c1 - c0], F32, name="gated%d" % c0, align_bytes=64)
             entries = offsets[:, c0 // PER_COL : c1 // PER_COL]
             nc.vector.tensor_tensor(gated[:], gate_win[:].indirect(entries), biased[:, c0:c1], MULT)
-            nc.sync.dma_start(out[:, c0:c1], gated[:])
+            halves = 2 if c0 == 0 else 1
+            width = (c1 - c0) // halves
+            for h in range(halves):
+                nc.sync.dma_start(out[:, c0 + h * width : c0 + (h + 1) * width], gated[:, h * width : (h + 1) * width])

from contextlib import ExitStack

import concourse.mybir as mybir

K, M, T, S = 1536, 128, 4096, 1536
FLOPS = 2 * K * M * S

F32 = mybir.dt.float32
BF16 = mybir.dt.bfloat16
I32 = mybir.dt.int32
U32 = mybir.dt.uint32
U16 = mybir.dt.uint16
U8 = mybir.dt.uint8
FP8X4 = mybir.dt.float8_e4m3fn_x4
FP4X4 = mybir.dt.float4_e2m1fn_x4
IDENT = mybir.ActivationFunctionType.Identity
MULT = mybir.AluOpType.mult

P = 128
PACK = 4
PASSES = 3
N_TILE = 512
PER_COL = 16
EARLY = 1024
N_LATE = 128
FIRST = 768
GATE_CUTS = (0, FIRST, 1280, 1536)


def tile_list_tabgate_bias_kernel(
    tc, tab_words, tab_scales, w8, w4_words, w4_scales, gT, b, offs, out
):
    nc = tc.nc
    with ExitStack() as ctx:
        keep = ctx.enter_context(tc.tile_pool(name="keep", bufs=1))
        shared = ctx.enter_context(tc.tile_pool(name="shared", bufs=1))
        psum = ctx.enter_context(tc.psum_pool(name="psum", bufs=1))

        offsets = keep.tile([P, S // PER_COL], U16, name="offsets")
        scale_win = shared.tile([P, T // 4], I32, name="scale_win", offset=4 * T - 1024, align_bytes=64)
        w8_raw = keep.tile([P, PACK, M], F32, name="w8_raw", align_bytes=64)
        w8_bf = keep.tile([P, M, PACK], BF16, name="w8_bf", align_bytes=64)
        word_win = [
            keep.tile([P, T], I32, name="word_win0", tag="slot_b", align_bytes=64),
            keep.tile([P, T], I32, name="word_win1", tag="slot_c", align_bytes=64),
        ]
        w8_codes = keep.tile([P, M], U32, name="w8_codes", align_bytes=64)
        w8_scales = keep.tile([P, M], U8, name="w8_scales", align_bytes=64)
        w4_planes = keep.tile([P, 2, M // 4], I32, name="w4_planes", align_bytes=64)
        bias_rows = keep.tile([P, 32], F32, name="bias_rows", align_bytes=64)
        bias = keep.tile([P, 32], F32, name="bias", align_bytes=64)
        picked_rows = keep.tile([P, S // 4], I32, name="picked_rows", align_bytes=64)
        early_planes = keep.tile([P, EARLY // 4], I32, name="early_planes", align_bytes=64)
        last_plane = keep.tile([P, EARLY // 4], I32, name="last_plane", align_bytes=64)
        picked = [keep.tile([P, S], U32, name="picked%d" % a, align_bytes=64) for a in range(PASSES)]
        biased = keep.tile([P, S], F32, name="biased", align_bytes=64)
        banks = [(0, N_TILE), (N_TILE, FIRST), (FIRST, EARLY)] + [(c, c + N_LATE) for c in range(EARLY, S, N_LATE)]
        acc = [psum.tile([P, N_TILE], F32, name="acc%d" % i) for i in range(len(banks))]

        words = [tab_words[a].rearrange("p t i -> p (t i)").bitcast(I32) for a in range(PASSES)]

        nc.gpsimd.memset(bias_rows[:], 0.0)
        nc.gpsimd.memset(w4_planes[:], 0)
        nc.vector.memset(scale_win[:], 0)
        nc.vector.memset(last_plane[:], 0)

        w4_rows = w4_scales.bitcast(I32).rearrange("a (q r) n -> r q a n", r=4)
        nc.sync.dma_start(offsets[:], offs)
        nc.sync.dma_start(word_win[0][0:P:2, :], words[0][0:P:2, :])
        nc.sync.dma_start(bias_rows[0:P:32, :], b.rearrange("(q i) -> q i", i=32))
        for r in range(2):
            nc.sync.dma_start(w4_planes[r:P:32, :, :], w4_rows[r])
        place_of = (2, 0, 1)
        for a in range(PASSES):
            nc.sync.dma_start(scale_win[32 + place_of[a] : 96 : 4, :], tab_scales[a].bitcast(I32))
        nc.sync.dma_start(word_win[0][1:P:2, :], words[0][1:P:2, :])
        nc.sync.dma_start(w8_raw[:], w8.rearrange("(p j) n -> p j n", j=PACK))
        for r in range(2, 4):
            nc.sync.dma_start(w4_planes[r:P:32, :, :], w4_rows[r])
        nc.sync.dma_start(word_win[1][:], words[1])

        nc.scalar.copy(w8_bf[:], w8_raw[:].rearrange("p j n -> p n j"))
        nc.vector.quantize_mx(
            out=w8_codes[:].bitcast(FP8X4), scales=w8_scales[:], in_=w8_bf[:].rearrange("p n j -> p (n j)")
        )

        nc.vector.transpose(bias[:], bias_rows[:])
        nc.vector.tensor_copy(picked_rows[:].bitcast(U8), scale_win[:].bitcast(U8).indirect(offsets[:]))
        word_win.append(shared.tile([P, T], I32, name="word_win2", offset=0, align_bytes=64))
        w4_codes = shared.tile([P, 2, 2 * M], U8, name="w4_codes", offset=4 * T, align_bytes=64)
        for r in range(4):
            nc.sync.dma_start(last_plane[r:P:32, :], picked_rows[33 + 4 * r : 96 : 16, : EARLY // 4])
        nc.sync.dma_start(word_win[2][:], words[2])
        nc.sync.dma_start(w4_codes[:].bitcast(I32), w4_words.rearrange("a p n -> p a n").bitcast(I32))
        for r in range(4):
            nc.sync.dma_start(early_planes[r:P:4, :], picked_rows[32 + 4 * r : 96 + 4 * r : 2, : EARLY // 4])

        nc.vector.tensor_copy(picked[0][:], word_win[0][:].bitcast(U32).indirect(offsets[:]))
        gate_win = keep.tile([P, T], F32, name="gate_win", tag="slot_b", align_bytes=64)
        nc.sync.dma_start(gate_win[:], gT)
        nc.vector.tensor_copy(picked[1][:], word_win[1][:].bitcast(U32).indirect(offsets[:]))

        late_planes = keep.tile([P, 2, (S - EARLY) // 4], I32, name="late_planes", tag="slot_c", align_bytes=64)
        for r in range(4):
            nc.sync.dma_start(late_planes[r:P:4, :, :], picked_rows[32 + 4 * r : 96 + 4 * r, EARLY // 4 :])

        def passes(a, i, first, last):
            b0, b1 = banks[i]
            width = N_TILE if b1 - b0 == N_TILE else N_LATE
            if a == 0:
                lhsT, lhsT_scale = w8_codes[:].bitcast(FP8X4), w8_scales[:]
            else:
                lhsT, lhsT_scale = w4_codes[:, a - 1, :].bitcast(FP4X4), w4_planes[:, a - 1, :].bitcast(U8)
            for c0 in range(b0, b1, width):
                c1 = c0 + width
                k = 4 if a == 0 else 0
                if c0 >= EARLY:
                    plane = late_planes[k:P, a // 2, (c0 - EARLY) // 4 : (c1 - EARLY) // 4]
                elif a == 2:
                    plane = last_plane[:, c0 // 4 : c1 // 4]
                else:
                    plane = early_planes[k:P, c0 // 4 : c1 // 4]
                nc.tensor.matmul_mx(
                    out=acc[i][:, c0 - b0 : c1 - b0],
                    lhsT=lhsT,
                    lhsT_scale=lhsT_scale,
                    rhs=picked[a][:, c0:c1].bitcast(FP8X4),
                    rhs_scale=plane.bitcast(U8),
                    start=(first and c0 == b0),
                    stop=(last and c1 == b1),
                )

        def add_bias(i):
            b0, b1 = banks[i]
            nc.scalar.activation(biased[:, b0:b1], acc[i][:, : b1 - b0], IDENT, bias=bias[:, 0:1])

        def pick_last_words(c0, c1):
            entries = offsets[:, c0 // PER_COL : c1 // PER_COL]
            nc.vector.tensor_copy(picked[2][:, c0:c1], word_win[2][:].bitcast(U32).indirect(entries))

        for c0 in range(0, S, N_TILE):
            pick_last_words(c0, c0 + N_TILE)
        for i in range(len(banks)):
            order = (0, 2, 1) if i < 3 else (2, 0, 1)
            for a in order:
                passes(a, i, a == order[0], a == order[-1])
            add_bias(i)

        for c0, c1 in zip(GATE_CUTS[:-1], GATE_CUTS[1:]):
            gated = keep.tile([P, c1 - c0], F32, name="gated%d" % c0, align_bytes=64)
            entries = offsets[:, c0 // PER_COL : c1 // PER_COL]
            nc.vector.tensor_tensor(gated[:], gate_win[:].indirect(entries), biased[:, c0:c1], MULT)
            halves = 2 if c0 == 0 else 1
            width = (c1 - c0) // halves
            for h in range(halves):
                nc.sync.dma_start(out[:, c0 + h * width : c0 + (h + 1) * width], gated[:, h * width : (h + 1) * width])
